import numpy as np
import ml_dtypes


def mxq(x, axis, fmt="e4m3"):
    dtype, down = {"e4m3": (ml_dtypes.float8_e4m3fn, 7), "e5m2": (ml_dtypes.float8_e5m2, 14)}[fmt]
    v = np.moveaxis(np.asarray(x, np.float32).astype(ml_dtypes.bfloat16).astype(np.float64), axis, -1)
    blocks = v.reshape(v.shape[:-1] + (-1, 32))
    amax = np.abs(blocks).max(-1, keepdims=True)
    byte = np.maximum(np.where(amax > 0, np.frexp(amax)[1] - 1 + 127, 0) - down, 1)
    scale = np.exp2(byte - 127.0)
    codes = (blocks / scale).astype(np.float32).astype(dtype).astype(np.float64)
    return np.moveaxis((codes * scale).reshape(v.shape), -1, axis)


WIDE = False


def mx_kscale(k, group=512):
    if not WIDE:
        return np.ones(k)
    levels = np.array([10, -10, 5, -5, 0])
    if group != 512:
        return np.exp2(np.random.permutation(np.resize(levels, k // group))).repeat(group)
    if k % 512:
        return np.exp2(np.random.permutation(np.resize(levels, k // 32))).repeat(32)
    a = np.empty((k // 512, 16))
    for p in range(k // 512):
        a[p, :8] = np.random.permutation(np.resize(levels, 8))
        for g in range(8):
            far = levels[np.abs(levels - a[p, g]) >= 10]
            a[p, g + 8] = far[np.random.randint(len(far))]
    return np.exp2(a.ravel()).repeat(32)


def f64(x):
    return np.asarray(x).astype(np.float64)


def striped(idx):
    return np.tile(np.asarray(idx).reshape(-1, 16).T, (8, 1)).astype(np.uint16)


def unstriped(offs):
    return offs[:16].T.reshape(-1).astype(np.int64)


H, KV, D, NQ, N = 4, 4, 128, 512, 1024
CAP = 2.0


def setup_inputs():
    n = np.random.standard_normal
    s = mx_kscale(D, 0)[:, None]
    u = mx_kscale(N)
    t = np.random.uniform(0.5, 2.0, N) * u
    v = n((KV, N, 128))
    return {
        "qT": (n((H, D, NQ)) * s * (0.70 / np.sqrt(D))).astype(np.float32),
        "kT": (n((KV, D, N)) / s).astype(np.float32),
        "t": t.reshape(N, 1).astype(np.float32),
        "v": (v / t[:, None]).astype(np.float32),
        "mask": (np.arange(N)[:, None] <= np.sort(np.random.randint(N // 4, N, NQ))[None, :]).astype(np.float32),
        "og": n((H, NQ, 128)).astype(np.float32),
    }


def reference(qT, kT, t, v, mask, og):
    a = mxq(f64(kT), 1, "e4m3").transpose(0, 2, 1) @ mxq(f64(qT), 1, "e4m3")
    a = CAP * np.tanh(a / CAP)
    p = a / (1.0 + np.exp(-a))
    p = p * f64(mask)
    w = p * f64(t)
    y = mxq(w, 1, "e4m3").transpose(0, 2, 1) @ mxq(f64(v), 1, "e4m3")
    y = y / 16.0
    y = y / (1.0 + np.exp(-f64(og)))
    return y

@@ -1,0 +1,265 @@
+from contextlib import ExitStack
+
+import concourse.mybir as mybir
+
+H, D, NQ, N, E = 4, 128, 512, 1024, 128
+FLOPS = 2 * H * N * NQ * D + 2 * H * NQ * N * E
+
+F32 = mybir.dt.float32
+BF16 = mybir.dt.bfloat16
+U32 = mybir.dt.uint32
+U8 = mybir.dt.uint8
+FP8X4 = mybir.dt.float8_e4m3fn_x4
+ACT = mybir.ActivationFunctionType
+ALU = mybir.AluOpType
+
+P = 128
+PACK = 4
+ROWS = D // PACK
+PASS = P * PACK
+PASSES = N // PASS
+QC = 128
+CHUNKS = NQ // QC
+TANH_RING = 3
+SILU_RING = 8
+W_RING = 3
+Y_BANKS = 4
+
+
+def tile_rows_a_silu_mask_cap_gate_kernel(tc, qT, kT, t, v, mask, og, out):
+    nc = tc.nc
+    with ExitStack() as ctx:
+        sb = ctx.enter_context(tc.tile_pool(name="sb", bufs=1))
+        ps = ctx.enter_context(tc.psum_pool(name="ps", bufs=1))
+        ctx.enter_context(tc.manual_schedule())
+
+        def sbuf(name, shape, dtype):
+            return sb.tile(shape, dtype, name=name, align_bytes=64)
+
+        q_hbm = qT.rearrange("h (p j) n -> (h p) j n", j=PACK)
+        k_hbm = kT.rearrange("h (p j) n -> (h p) j n", j=PACK)
+        m_hbm = mask.rearrange("(c p j) q -> c p j q", p=P, j=PACK)
+        v_hbm = v.rearrange("h (c p j) e -> c p h (j e)", p=P, j=PACK)
+
+        half = PASS // 2
+        q_first = sbuf("q_first", [P, PACK, QC], F32)
+        q_rest = sbuf("q_rest", [P, PACK, NQ - QC], F32)
+        k0_lo = sbuf("k0_lo", [P, PACK, half], F32)
+        k0_hi = sbuf("k0_hi", [P, PACK, half], F32)
+        k1_raw = sbuf("k1_raw", [P, PACK, PASS], F32)
+        m0_lo = sbuf("m0_lo", [P, PACK, NQ // 2], F32)
+        m0_hi = sbuf("m0_hi", [P, PACK, NQ // 2], F32)
+        m1_raw = sbuf("m1_raw", [P, PACK, NQ], F32)
+        v_raw = [sbuf("v_raw%d" % c, [P, H, PACK * E], F32) for c in range(PASSES)]
+        og_raw = sbuf("og_raw", [P, H * CHUNKS, E], F32)
+        t_sb = sbuf("t_sb", [P, PASSES, PACK], F32)
+
+        nc.scalar.dma_start(out=t_sb[:], in_=t.rearrange("(c p j) o -> p c (j o)", p=P, j=PACK))
+        nc.sync.dma_start(out=k0_lo[:], in_=k_hbm[:, :, 0:half])
+        nc.sync.dma_start(out=k0_hi[:], in_=k_hbm[:, :, half:PASS])
+        nc.sync.dma_start(out=q_first[:], in_=q_hbm[:, :, 0:QC])
+        nc.sync.dma_start(out=q_rest[:], in_=q_hbm[:, :, QC:NQ])
+        nc.sync.dma_start(out=m0_lo[:], in_=m_hbm[0][:, :, 0 : NQ // 2])
+        nc.sync.dma_start(out=m0_hi[:], in_=m_hbm[0][:, :, NQ // 2 : NQ])
+        nc.sync.dma_start(out=k1_raw[:], in_=k_hbm[:, :, PASS:N])
+        nc.sync.dma_start(out=m1_raw[:], in_=m_hbm[1])
+        for c in range(PASSES):
+            nc.sync.dma_start(out=v_raw[c][:], in_=v_hbm[c])
+        nc.sync.dma_start(out=og_raw[:], in_=og.rearrange("h (c p) e -> p (h c) e", p=QC))
+
+        q_bf = sbuf("q_bf", [P, NQ * PACK], BF16)
+        k_bf = [sbuf("k_bf%d" % c, [P, PASS * PACK], BF16) for c in range(PASSES)]
+        v_bf = [sbuf("v_bf%d" % c, [P, H * E * PACK], BF16) for c in range(PASSES)]
+        q_codes = sbuf("q_codes", [P, NQ], U32)
+        q_scales = sbuf("q_scales", [P, NQ], U8)
+        k_codes = sbuf("k_codes", [P, N], U32)
+        k_scales = sbuf("k_scales", [P, N], U8)
+        v_codes = sbuf("v_codes", [P, PASSES * H * E], U32)
+        v_scales = sbuf("v_scales", [P, PASSES * H * E], U8)
+        w_codes = sbuf("w_codes", [P, PASSES * CHUNKS * H * QC], U32)
+        w_scales = sbuf("w_scales", [P, PASSES * CHUNKS * H * QC], U8)
+        mt_rows = [sbuf("mt_rows%d" % c, [P, PACK, NQ], F32) for c in range(PASSES)]
+        mt = [sbuf("mt%d" % c, [P, NQ * PACK], F32) for c in range(PASSES)]
+        gate = sbuf("gate", [P, CHUNKS, H * E], F32)
+        tanh_ring = [sbuf("tanh%d" % i, [P, 2, QC * PACK], F32) for i in range(TANH_RING)]
+        silu_ring = [sbuf("silu%d" % i, [P, 2, QC * PACK], F32) for i in range(SILU_RING)]
+        w_ring = [sbuf("w%d" % i, [P, 2 * QC * PACK], BF16) for i in range(W_RING)]
+        score_bank = [ps.tile([P, PACK * QC], F32, name="score%d" % h) for h in range(H)]
+        y_bank = [ps.tile([P, PACK * QC], F32, name="y%d" % i) for i in range(Y_BANKS)]
+
+        def quantize(codes, scales, values, first, width):
+            nc.vector.quantize_mx(
+                out=codes[:, first : first + width].bitcast(FP8X4),
+                scales=scales[:, first : first + width],
+                in_=values,
+            )
+
+        def interleave(dst, src):
+            nc.vector.tensor_copy(
+                out=dst.rearrange("p (c i j) -> p c j i", i=4, j=PACK),
+                in_=src.rearrange("p j (c i) -> p c j i", i=4),
+            )
+
+        def deal_keys(c, src, s0, s1):
+            dst = k_bf[c][:].rearrange("p (r s j) -> p s j r", r=PACK, j=PACK)
+            nc.vector.tensor_copy(out=dst[:, s0:s1], in_=src.rearrange("p j (s r) -> p s j r", r=PACK))
+
+        def quantize_keys(c, r0, r1):
+            quantize(k_codes, k_scales, k_bf[c][:, r0 * P * PACK : r1 * P * PACK], c * PASS + r0 * P, (r1 - r0) * P)
+
+        def scale_mask(c, src, q0, q1):
+            for j in range(PACK):
+                nc.vector.tensor_scalar(
+                    out=mt_rows[c][:, j, q0:q1], in0=src[:, j, :], scalar1=t_sb[:, c, j : j + 1],
+                    scalar2=1.0 / 32.0, op0=ALU.mult, op1=ALU.mult,
+                )
+
+        def interleave_mask(c, q0, q1):
+            interleave(mt[c][:, q0 * PACK : q1 * PACK], mt_rows[c][:, :, q0:q1])
+
+        def interleave_values(c):
+            nc.vector.tensor_copy(
+                out=v_bf[c][:].rearrange("p (h c i j) -> p h c j i", h=H, i=4, j=PACK),
+                in_=v_raw[c][:].rearrange("p h (j c i) -> p h c j i", j=PACK, i=4),
+            )
+
+        def quantize_values(c):
+            quantize(v_codes, v_scales, v_bf[c][:], c * H * E, H * E)
+
+        units = [(c, qc, h) for c in range(PASSES) for qc in range(CHUNKS) for h in range(H)]
+        jobs = [[u, u + 1] for u in range(0, len(units) - 2, 2)] + [[len(units) - 2], [len(units) - 1]]
+
+        def scores(u):
+            c, qc, h = units[u]
+            rows = slice(ROWS * h, ROWS * (h + 1))
+            q_cols = slice(qc * QC, (qc + 1) * QC)
+            for r in range(PACK):
+                k_cols = slice(c * PASS + r * P, c * PASS + (r + 1) * P)
+                nc.tensor.matmul_mx(
+                    out=score_bank[h][:, r * QC : (r + 1) * QC],
+                    lhsT=k_codes[rows, k_cols].bitcast(FP8X4), lhsT_scale=k_scales[rows, k_cols],
+                    rhs=q_codes[rows, q_cols].bitcast(FP8X4), rhs_scale=q_scales[rows, q_cols],
+                    start=True, stop=True,
+                )
+
+        def cap(g, place):
+            h = units[jobs[g][place]][2]
+            nc.scalar.activation(
+                out=tanh_ring[g % TANH_RING][:, place, :].rearrange("p (n r) -> p n r", r=PACK),
+                in_=score_bank[h][:].rearrange("p (r n) -> p n r", r=PACK),
+                func=ACT.Tanh, scale=0.5,
+            )
+
+        def silu(g):
+            n = len(jobs[g])
+            nc.scalar.activation(
+                out=silu_ring[g % SILU_RING][:, 0:n, :], in_=tanh_ring[g % TANH_RING][:, 0:n, :],
+                func=ACT.Silu, scale=2.0,
+            )
+
+        def weigh(g):
+            n = len(jobs[g])
+            c, qc, h = units[jobs[g][0]]
+            width = QC * PACK
+            nc.vector.tensor_tensor(
+                out=w_ring[g % W_RING][:, 0 : n * width].rearrange("p (a x) -> p a x", a=n),
+                in0=silu_ring[g % SILU_RING][:, 0:n, :],
+                in1=mt[c][:, qc * width : (qc + 1) * width].unsqueeze(1).to_broadcast([P, n, width]),
+                op=ALU.mult,
+            )
+
+        def quantize_weights(g):
+            n = len(jobs[g])
+            quantize(w_codes, w_scales, w_ring[g % W_RING][:, 0 : n * QC * PACK], jobs[g][0] * QC, n * QC)
+
+        def second_product(g):
+            for place, u in enumerate(jobs[g]):
+                c_last, qc, h = units[u]
+                for c in range(PASSES):
+                    w0 = ((c * CHUNKS + qc) * H + h) * QC
+                    v0 = (c * H + h) * E
+                    nc.tensor.matmul_mx(
+                        out=y_bank[g % Y_BANKS][:, place * E : (place + 1) * E],
+                        lhsT=w_codes[:, w0 : w0 + QC].bitcast(FP8X4), lhsT_scale=w_scales[:, w0 : w0 + QC],
+                        rhs=v_codes[:, v0 : v0 + E].bitcast(FP8X4), rhs_scale=v_scales[:, v0 : v0 + E],
+                        start=(c == 0), stop=(c == PASSES - 1),
+                    )
+
+        def make_gate(qc):
+            nc.scalar.activation(
+                out=gate[:, qc, :].rearrange("p (h e) -> p h e", h=H),
+                in_=og_raw[:].rearrange("p (h c) e -> p c h e", h=H)[:, qc],
+                func=ACT.Tanh, scale=0.5,
+            )
+
+        def finish(g):
+            n = len(jobs[g])
+            c, qc, h = units[jobs[g][0]]
+            result = sbuf("result%d" % g, [P, n * E], F32)
+            nc.vector.scalar_tensor_tensor(
+                out=result[:], in0=gate[:, qc, h * E : (h + n) * E], scalar=1.0,
+                in1=y_bank[g % Y_BANKS][:, 0 : n * E], op0=ALU.add, op1=ALU.mult,
+            )
+            nc.sync.dma_start(
+                out=out[h : h + n, qc * QC : (qc + 1) * QC, :].rearrange("h q e -> q h e"),
+                in_=result[:].rearrange("p (h e) -> p h e", h=n),
+            )
+
+        nc.scalar.copy(
+            out=q_bf[:, 0 : QC * PACK].rearrange("p (c i j) -> p c j i", i=4, j=PACK),
+            in_=q_first[:].rearrange("p j (c i) -> p c j i", i=4),
+        )
+        deal_keys(0, k0_lo[:], 0, P // 2)
+        deal_keys(0, k0_hi[:], P // 2, P)
+        quantize_keys(0, 0, 2)
+        quantize(q_codes, q_scales, q_bf[:, 0 : QC * PACK], 0, QC)
+        quantize_keys(0, 2, 4)
+        for u in range(H):
+            scores(u)
+        interleave(q_bf[:, QC * PACK : NQ * PACK], q_rest[:])
+        quantize(q_codes, q_scales, q_bf[:, QC * PACK : 2 * QC * PACK], QC, QC)
+        quantize(q_codes, q_scales, q_bf[:, 2 * QC * PACK : NQ * PACK], 2 * QC, 2 * QC)
+        scale_mask(0, m0_lo, 0, NQ // 2)
+        interleave_mask(0, 0, NQ // 2)
+
+        side = [
+            lambda: scale_mask(0, m0_hi, NQ // 2, NQ),
+            lambda: interleave_mask(0, NQ // 2, NQ),
+            lambda: deal_keys(1, k1_raw[:, :, 0:half], 0, P // 2),
+            lambda: deal_keys(1, k1_raw[:, :, half:PASS], P // 2, P),
+            lambda: quantize_keys(1, 0, 4),
+            lambda: scale_mask(1, m1_raw, 0, NQ),
+            lambda: interleave_mask(1, 0, NQ // 2),
+            lambda: interleave_mask(1, NQ // 2, NQ),
+            lambda: interleave_values(0),
+            lambda: quantize_values(0),
+            lambda: interleave_values(1),
+            lambda: quantize_values(1),
+        ]
+        first_last_pass_job = len(units) // PASSES // 2
+        n_jobs = len(jobs)
+        for i in range(n_jobs + 3):
+            places = range(len(jobs[i])) if i < n_jobs else range(0)
+            for place in places:
+                cap(i, place)
+                u_next = jobs[i][place] + H
+                if u_next < len(units):
+                    scores(u_next)
+                if place == 0 and i >= 1:
+                    silu(i - 1)
+            if i == n_jobs:
+                silu(i - 1)
+            if first_last_pass_job <= i < first_last_pass_job + CHUNKS:
+                make_gate(i - first_last_pass_job)
+            if 1 <= i <= n_jobs:
+                weigh(i - 1)
+            if i >= 1 and 2 * (i - 1) < len(side):
+                side[2 * (i - 1)]()
+            if 2 <= i <= n_jobs + 1:
+                quantize_weights(i - 2)
+            if i >= 1 and 2 * (i - 1) + 1 < len(side):
+                side[2 * (i - 1) + 1]()
+            if first_last_pass_job <= i - 3 < n_jobs:
+                finish(i - 3)
+            if first_last_pass_job <= i - 2 < n_jobs:
+                second_product(i - 2)

@@ -21,7 +21,7 @@ PASSES = N // PASS
 QC = 128
 CHUNKS = NQ // QC
 TANH_RING = 3
-SILU_RING = 8
+SILU_RING = 4
 W_RING = 3
 Y_BANKS = 4
 
@@ -78,12 +78,12 @@ def tile_rows_a_silu_mask_cap_gate_kernel(tc, qT, kT, t, v, mask, og, out):
         v_scales = sbuf("v_scales", [P, PASSES * H * E], U8)
         w_codes = sbuf("w_codes", [P, PASSES * CHUNKS * H * QC], U32)
         w_scales = sbuf("w_scales", [P, PASSES * CHUNKS * H * QC], U8)
-        mt_rows = [sbuf("mt_rows%d" % c, [P, PACK, NQ], F32) for c in range(PASSES)]
+        mt_rows = sbuf("mt_rows", [P, PACK, NQ], F32)
         mt = [sbuf("mt%d" % c, [P, NQ * PACK], F32) for c in range(PASSES)]
         gate = sbuf("gate", [P, CHUNKS, H * E], F32)
-        tanh_ring = [sbuf("tanh%d" % i, [P, 2, QC * PACK], F32) for i in range(TANH_RING)]
-        silu_ring = [sbuf("silu%d" % i, [P, 2, QC * PACK], F32) for i in range(SILU_RING)]
-        w_ring = [sbuf("w%d" % i, [P, 2 * QC * PACK], BF16) for i in range(W_RING)]
+        tanh_ring = [sbuf("tanh%d" % i, [P, H, QC * PACK], F32) for i in range(TANH_RING)]
+        silu_ring = [sbuf("silu%d" % i, [P, H, QC * PACK], F32) for i in range(SILU_RING)]
+        w_ring = [sbuf("w%d" % i, [P, H * QC * PACK], BF16) for i in range(W_RING)]
         score_bank = [ps.tile([P, PACK * QC], F32, name="score%d" % h) for h in range(H)]
         y_bank = [ps.tile([P, PACK * QC], F32, name="y%d" % i) for i in range(Y_BANKS)]
 
@@ -110,12 +110,12 @@ def tile_rows_a_silu_mask_cap_gate_kernel(tc, qT, kT, t, v, mask, og, out):
         def scale_mask(c, src, q0, q1):
             for j in range(PACK):
                 nc.vector.tensor_scalar(
-                    out=mt_rows[c][:, j, q0:q1], in0=src[:, j, :], scalar1=t_sb[:, c, j : j + 1],
+                    out=mt_rows[:, j, q0:q1], in0=src[:, j, :], scalar1=t_sb[:, c, j : j + 1],
                     scalar2=1.0 / 32.0, op0=ALU.mult, op1=ALU.mult,
                 )
 
         def interleave_mask(c, q0, q1):
-            interleave(mt[c][:, q0 * PACK : q1 * PACK], mt_rows[c][:, :, q0:q1])
+            interleave(mt[c][:, q0 * PACK : q1 * PACK], mt_rows[:, :, q0:q1])
 
         def interleave_values(c):
             nc.vector.tensor_copy(
@@ -127,7 +127,8 @@ def tile_rows_a_silu_mask_cap_gate_kernel(tc, qT, kT, t, v, mask, og, out):
             quantize(v_codes, v_scales, v_bf[c][:], c * H * E, H * E)
 
         units = [(c, qc, h) for c in range(PASSES) for qc in range(CHUNKS) for h in range(H)]
-        jobs = [[u, u + 1] for u in range(0, len(units) - 2, 2)] + [[len(units) - 2], [len(units) - 1]]
+        sizes = [2, 2] + [H] * (PASSES * CHUNKS - 3) + [2, 2] + [1] * H
+        jobs = [list(range(sum(sizes[:g]), sum(sizes[: g + 1]))) for g in range(len(sizes))]
 
         def scores(u):
             c, qc, h = units[u]
@@ -185,10 +186,12 @@ def tile_rows_a_silu_mask_cap_gate_kernel(tc, qT, kT, t, v, mask, og, out):
                         start=(c == 0), stop=(c == PASSES - 1),
                     )
 
-        def make_gate(qc):
+        def make_gate(g):
+            n = len(jobs[g])
+            c, qc, h = units[jobs[g][0]]
             nc.scalar.activation(
-                out=gate[:, qc, :].rearrange("p (h e) -> p h e", h=H),
-                in_=og_raw[:].rearrange("p (h c) e -> p c h e", h=H)[:, qc],
+                out=gate[:, qc, h * E : (h + n) * E].rearrange("p (h e) -> p h e", h=n),
+                in_=og_raw[:].rearrange("p (h c) e -> p c h e", h=H)[:, qc, h : h + n],
                 func=ACT.Tanh, scale=0.5,
             )
 
@@ -212,32 +215,27 @@ def tile_rows_a_silu_mask_cap_gate_kernel(tc, qT, kT, t, v, mask, og, out):
         deal_keys(0, k0_lo[:], 0, P // 2)
         deal_keys(0, k0_hi[:], P // 2, P)
         quantize_keys(0, 0, 2)
-        quantize(q_codes, q_scales, q_bf[:, 0 : QC * PACK], 0, QC)
         quantize_keys(0, 2, 4)
+        quantize(q_codes, q_scales, q_bf[:, 0 : QC * PACK], 0, QC)
         for u in range(H):
             scores(u)
-        interleave(q_bf[:, QC * PACK : NQ * PACK], q_rest[:])
+        interleave(q_bf[:, QC * PACK : 2 * QC * PACK], q_rest[:, :, 0:QC])
+        interleave(q_bf[:, 2 * QC * PACK : NQ * PACK], q_rest[:, :, QC : NQ - QC])
         quantize(q_codes, q_scales, q_bf[:, QC * PACK : 2 * QC * PACK], QC, QC)
-        quantize(q_codes, q_scales, q_bf[:, 2 * QC * PACK : NQ * PACK], 2 * QC, 2 * QC)
         scale_mask(0, m0_lo, 0, NQ // 2)
+        quantize(q_codes, q_scales, q_bf[:, 2 * QC * PACK : NQ * PACK], 2 * QC, 2 * QC)
         interleave_mask(0, 0, NQ // 2)
+        scale_mask(0, m0_hi, NQ // 2, NQ)
 
         side = [
-            lambda: scale_mask(0, m0_hi, NQ // 2, NQ),
-            lambda: interleave_mask(0, NQ // 2, NQ),
-            lambda: deal_keys(1, k1_raw[:, :, 0:half], 0, P // 2),
-            lambda: deal_keys(1, k1_raw[:, :, half:PASS], P // 2, P),
-            lambda: quantize_keys(1, 0, 4),
-            lambda: scale_mask(1, m1_raw, 0, NQ),
-            lambda: interleave_mask(1, 0, NQ // 2),
-            lambda: interleave_mask(1, NQ // 2, NQ),
-            lambda: interleave_values(0),
-            lambda: quantize_values(0),
-            lambda: interleave_values(1),
-            lambda: quantize_values(1),
+            (lambda: interleave_mask(0, NQ // 2, NQ),),
+            (lambda: deal_keys(1, k1_raw[:], 0, P), lambda: quantize_keys(1, 0, PACK)),
+            (lambda: scale_mask(1, m1_raw, 0, NQ), lambda: interleave_mask(1, 0, NQ)),
+            (lambda: interleave_values(0), lambda: quantize_values(0)),
+            (lambda: interleave_values(1), lambda: quantize_values(1)),
         ]
-        first_last_pass_job = len(units) // PASSES // 2
         n_jobs = len(jobs)
+        last_pass = [g for g in range(n_jobs) if units[jobs[g][0]][0] == PASSES - 1]
         for i in range(n_jobs + 3):
             places = range(len(jobs[i])) if i < n_jobs else range(0)
             for place in places:
@@ -249,17 +247,18 @@ def tile_rows_a_silu_mask_cap_gate_kernel(tc, qT, kT, t, v, mask, og, out):
                     silu(i - 1)
             if i == n_jobs:
                 silu(i - 1)
-            if first_last_pass_job <= i < first_last_pass_job + CHUNKS:
-                make_gate(i - first_last_pass_job)
+            if i - 2 in last_pass:
+                make_gate(i - 2)
+            extra = side[i - 1] if 1 <= i <= len(side) else ()
             if 1 <= i <= n_jobs:
                 weigh(i - 1)
-            if i >= 1 and 2 * (i - 1) < len(side):
-                side[2 * (i - 1)]()
+            for step in extra[:1]:
+                step()
             if 2 <= i <= n_jobs + 1:
                 quantize_weights(i - 2)
-            if i >= 1 and 2 * (i - 1) + 1 < len(side):
-                side[2 * (i - 1) + 1]()
-            if first_last_pass_job <= i - 3 < n_jobs:
+            for step in extra[1:]:
+                step()
+            if i - 3 in last_pass:
                 finish(i - 3)
-            if first_last_pass_job <= i - 2 < n_jobs:
+            if i - 2 in last_pass:
                 second_product(i - 2)

@@ -15,6 +15,7 @@ ALU = mybir.AluOpType
 
 P = 128
 PACK = 4
+RUN = 4
 ROWS = D // PACK
 PASS = P * PACK
 PASSES = N // PASS
@@ -41,26 +42,27 @@ def tile_rows_a_silu_mask_cap_gate_kernel(tc, qT, kT, t, v, mask, og, out):
         m_hbm = mask.rearrange("(c p j) q -> c p j q", p=P, j=PACK)
         v_hbm = v.rearrange("h (c p j) e -> c p h (j e)", p=P, j=PACK)
 
-        half = PASS // 2
+        half_pass = PASS // 2
+        half_q = NQ // 2
         q_first = sbuf("q_first", [P, PACK, QC], F32)
         q_rest = sbuf("q_rest", [P, PACK, NQ - QC], F32)
-        k0_lo = sbuf("k0_lo", [P, PACK, half], F32)
-        k0_hi = sbuf("k0_hi", [P, PACK, half], F32)
+        k0_lo = sbuf("k0_lo", [P, PACK, half_pass], F32)
+        k0_hi = sbuf("k0_hi", [P, PACK, half_pass], F32)
         k1_raw = sbuf("k1_raw", [P, PACK, PASS], F32)
-        m0_lo = sbuf("m0_lo", [P, PACK, NQ // 2], F32)
-        m0_hi = sbuf("m0_hi", [P, PACK, NQ // 2], F32)
+        m0_lo = sbuf("m0_lo", [P, PACK, half_q], F32)
+        m0_hi = sbuf("m0_hi", [P, PACK, half_q], F32)
         m1_raw = sbuf("m1_raw", [P, PACK, NQ], F32)
         v_raw = [sbuf("v_raw%d" % c, [P, H, PACK * E], F32) for c in range(PASSES)]
         og_raw = sbuf("og_raw", [P, H * CHUNKS, E], F32)
         t_sb = sbuf("t_sb", [P, PASSES, PACK], F32)
 
-        nc.scalar.dma_start(out=t_sb[:], in_=t.rearrange("(c p j) o -> p c (j o)", p=P, j=PACK))
-        nc.sync.dma_start(out=k0_lo[:], in_=k_hbm[:, :, 0:half])
-        nc.sync.dma_start(out=k0_hi[:], in_=k_hbm[:, :, half:PASS])
+        nc.sync.dma_start(out=k0_lo[:], in_=k_hbm[:, :, 0:half_pass])
+        nc.sync.dma_start(out=k0_hi[:], in_=k_hbm[:, :, half_pass:PASS])
         nc.sync.dma_start(out=q_first[:], in_=q_hbm[:, :, 0:QC])
+        nc.sync.dma_start(out=t_sb[:], in_=t.rearrange("(c p j) o -> p c (j o)", p=P, j=PACK))
         nc.sync.dma_start(out=q_rest[:], in_=q_hbm[:, :, QC:NQ])
-        nc.sync.dma_start(out=m0_lo[:], in_=m_hbm[0][:, :, 0 : NQ // 2])
-        nc.sync.dma_start(out=m0_hi[:], in_=m_hbm[0][:, :, NQ // 2 : NQ])
+        nc.sync.dma_start(out=m0_lo[:], in_=m_hbm[0][:, :, 0:half_q])
+        nc.sync.dma_start(out=m0_hi[:], in_=m_hbm[0][:, :, half_q:NQ])
         nc.sync.dma_start(out=k1_raw[:], in_=k_hbm[:, :, PASS:N])
         nc.sync.dma_start(out=m1_raw[:], in_=m_hbm[1])
         for c in range(PASSES):
@@ -85,7 +87,7 @@ def tile_rows_a_silu_mask_cap_gate_kernel(tc, qT, kT, t, v, mask, og, out):
         silu_ring = [sbuf("silu%d" % i, [P, H, QC * PACK], F32) for i in range(SILU_RING)]
         w_ring = [sbuf("w%d" % i, [P, H * QC * PACK], BF16) for i in range(W_RING)]
         score_bank = [ps.tile([P, PACK * QC], F32, name="score%d" % h) for h in range(H)]
-        y_bank = [ps.tile([P, PACK * QC], F32, name="y%d" % i) for i in range(Y_BANKS)]
+        y_bank = [ps.tile([P, H * E], F32, name="y%d" % i) for i in range(Y_BANKS)]
 
         def quantize(codes, scales, values, first, width):
             nc.vector.quantize_mx(
@@ -94,11 +96,17 @@ def tile_rows_a_silu_mask_cap_gate_kernel(tc, qT, kT, t, v, mask, og, out):
                 in_=values,
             )
 
-        def interleave(dst, src):
-            nc.vector.tensor_copy(
-                out=dst.rearrange("p (c i j) -> p c j i", i=4, j=PACK),
-                in_=src.rearrange("p j (c i) -> p c j i", i=4),
+        def interleave(copy, dst, src):
+            copy(
+                out=dst.rearrange("p (c i j) -> p c j i", i=RUN, j=PACK),
+                in_=src.rearrange("p j (c i) -> p c j i", i=RUN),
             )
+
+        def interleave_queries(copy, src, q0, q1):
+            interleave(copy, q_bf[:, q0 * PACK : q1 * PACK], src)
+
+        def quantize_queries(q0, q1):
+            quantize(q_codes, q_scales, q_bf[:, q0 * PACK : q1 * PACK], q0, q1 - q0)
 
         def deal_keys(c, src, s0, s1):
             dst = k_bf[c][:].rearrange("p (r s j) -> p s j r", r=PACK, j=PACK)
@@ -108,26 +116,26 @@ def tile_rows_a_silu_mask_cap_gate_kernel(tc, qT, kT, t, v, mask, og, out):
             quantize(k_codes, k_scales, k_bf[c][:, r0 * P * PACK : r1 * P * PACK], c * PASS + r0 * P, (r1 - r0) * P)
 
         def scale_mask(c, src, q0, q1):
-            for j in range(PACK):
+            for r in range(PACK):
                 nc.vector.tensor_scalar(
-                    out=mt_rows[:, j, q0:q1], in0=src[:, j, :], scalar1=t_sb[:, c, j : j + 1],
+                    out=mt_rows[:, r, q0:q1], in0=src[:, r, :], scalar1=t_sb[:, c, r : r + 1],
                     scalar2=1.0 / 32.0, op0=ALU.mult, op1=ALU.mult,
                 )
 
         def interleave_mask(c, q0, q1):
-            interleave(mt[c][:, q0 * PACK : q1 * PACK], mt_rows[:, :, q0:q1])
+            interleave(nc.vector.tensor_copy, mt[c][:, q0 * PACK : q1 * PACK], mt_rows[:, :, q0:q1])
 
         def interleave_values(c):
             nc.vector.tensor_copy(
-                out=v_bf[c][:].rearrange("p (h c i j) -> p h c j i", h=H, i=4, j=PACK),
-                in_=v_raw[c][:].rearrange("p h (j c i) -> p h c j i", j=PACK, i=4),
+                out=v_bf[c][:].rearrange("p (h c i r) -> p h c r i", h=H, i=RUN, r=PACK),
+                in_=v_raw[c][:].rearrange("p h (r c i) -> p h c r i", r=PACK, i=RUN),
             )
 
         def quantize_values(c):
             quantize(v_codes, v_scales, v_bf[c][:], c * H * E, H * E)
 
         units = [(c, qc, h) for c in range(PASSES) for qc in range(CHUNKS) for h in range(H)]
-        sizes = [2, 2] + [H] * (PASSES * CHUNKS - 3) + [2, 2] + [1] * H
+        sizes = [2, 2] + [H] * (PASSES * CHUNKS - 3) + [2, 2, 2, 1, 1]
         jobs = [list(range(sum(sizes[:g]), sum(sizes[: g + 1]))) for g in range(len(sizes))]
 
         def scores(u):
@@ -143,10 +151,10 @@ def tile_rows_a_silu_mask_cap_gate_kernel(tc, qT, kT, t, v, mask, og, out):
                     start=True, stop=True,
                 )
 
-        def cap(g, place):
-            h = units[jobs[g][place]][2]
+        def cap(g, member):
+            h = units[jobs[g][member]][2]
             nc.scalar.activation(
-                out=tanh_ring[g % TANH_RING][:, place, :].rearrange("p (n r) -> p n r", r=PACK),
+                out=tanh_ring[g % TANH_RING][:, member, :].rearrange("p (n r) -> p n r", r=PACK),
                 in_=score_bank[h][:].rearrange("p (r n) -> p n r", r=PACK),
                 func=ACT.Tanh, scale=0.5,
             )
@@ -174,13 +182,13 @@ def tile_rows_a_silu_mask_cap_gate_kernel(tc, qT, kT, t, v, mask, og, out):
             quantize(w_codes, w_scales, w_ring[g % W_RING][:, 0 : n * QC * PACK], jobs[g][0] * QC, n * QC)
 
         def second_product(g):
-            for place, u in enumerate(jobs[g]):
-                c_last, qc, h = units[u]
+            for member, u in enumerate(jobs[g]):
+                qc, h = units[u][1:]
                 for c in range(PASSES):
                     w0 = ((c * CHUNKS + qc) * H + h) * QC
                     v0 = (c * H + h) * E
                     nc.tensor.matmul_mx(
-                        out=y_bank[g % Y_BANKS][:, place * E : (place + 1) * E],
+                        out=y_bank[g % Y_BANKS][:, member * E : (member + 1) * E],
                         lhsT=w_codes[:, w0 : w0 + QC].bitcast(FP8X4), lhsT_scale=w_scales[:, w0 : w0 + QC],
                         rhs=v_codes[:, v0 : v0 + E].bitcast(FP8X4), rhs_scale=v_scales[:, v0 : v0 + E],
                         start=(c == 0), stop=(c == PASSES - 1),
@@ -208,27 +216,25 @@ def tile_rows_a_silu_mask_cap_gate_kernel(tc, qT, kT, t, v, mask, og, out):
                 in_=result[:].rearrange("p (h e) -> p h e", h=n),
             )
 
-        nc.scalar.copy(
-            out=q_bf[:, 0 : QC * PACK].rearrange("p (c i j) -> p c j i", i=4, j=PACK),
-            in_=q_first[:].rearrange("p j (c i) -> p c j i", i=4),
-        )
+        interleave_queries(nc.scalar.copy, q_first[:], 0, QC)
         deal_keys(0, k0_lo[:], 0, P // 2)
         deal_keys(0, k0_hi[:], P // 2, P)
-        quantize_keys(0, 0, 2)
-        quantize_keys(0, 2, 4)
-        quantize(q_codes, q_scales, q_bf[:, 0 : QC * PACK], 0, QC)
+        quantize_keys(0, 0, PACK // 2)
+        quantize_keys(0, PACK // 2, PACK)
+        quantize_queries(0, QC)
         for u in range(H):
             scores(u)
-        interleave(q_bf[:, QC * PACK : 2 * QC * PACK], q_rest[:, :, 0:QC])
-        interleave(q_bf[:, 2 * QC * PACK : NQ * PACK], q_rest[:, :, QC : NQ - QC])
-        quantize(q_codes, q_scales, q_bf[:, QC * PACK : 2 * QC * PACK], QC, QC)
-        scale_mask(0, m0_lo, 0, NQ // 2)
-        quantize(q_codes, q_scales, q_bf[:, 2 * QC * PACK : NQ * PACK], 2 * QC, 2 * QC)
-        interleave_mask(0, 0, NQ // 2)
-        scale_mask(0, m0_hi, NQ // 2, NQ)
 
-        side = [
-            (lambda: interleave_mask(0, NQ // 2, NQ),),
+        interleave_queries(nc.vector.tensor_copy, q_rest[:, :, 0:QC], QC, half_q)
+        interleave_queries(nc.vector.tensor_copy, q_rest[:, :, QC : NQ - QC], half_q, NQ)
+        quantize_queries(QC, half_q)
+        scale_mask(0, m0_lo, 0, half_q)
+        quantize_queries(half_q, NQ)
+        interleave_mask(0, 0, half_q)
+        scale_mask(0, m0_hi, half_q, NQ)
+
+        preparation = [
+            (lambda: interleave_mask(0, half_q, NQ),),
             (lambda: deal_keys(1, k1_raw[:], 0, P), lambda: quantize_keys(1, 0, PACK)),
             (lambda: scale_mask(1, m1_raw, 0, NQ), lambda: interleave_mask(1, 0, NQ)),
             (lambda: interleave_values(0), lambda: quantize_values(0)),
@@ -236,29 +242,32 @@ def tile_rows_a_silu_mask_cap_gate_kernel(tc, qT, kT, t, v, mask, og, out):
         ]
         n_jobs = len(jobs)
         last_pass = [g for g in range(n_jobs) if units[jobs[g][0]][0] == PASSES - 1]
+
         for i in range(n_jobs + 3):
-            places = range(len(jobs[i])) if i < n_jobs else range(0)
-            for place in places:
-                cap(i, place)
-                u_next = jobs[i][place] + H
+            members = range(len(jobs[i])) if i < n_jobs else range(0)
+            for member in members:
+                cap(i, member)
+                u_next = jobs[i][member] + H
                 if u_next < len(units):
                     scores(u_next)
-                if place == 0 and i >= 1:
+                if member == 0 and i - 2 in last_pass:
+                    second_product(i - 2)
+                if member == 0 and i >= 1:
                     silu(i - 1)
+            if i >= n_jobs and i - 2 in last_pass:
+                second_product(i - 2)
             if i == n_jobs:
                 silu(i - 1)
-            if i - 2 in last_pass:
-                make_gate(i - 2)
-            extra = side[i - 1] if 1 <= i <= len(side) else ()
+            if i - 3 in last_pass:
+                make_gate(i - 3)
+            extra = preparation[i - 1] if 1 <= i <= len(preparation) else ()
             if 1 <= i <= n_jobs:
                 weigh(i - 1)
-            for step in extra[:1]:
-                step()
-            if 2 <= i <= n_jobs + 1:
-                quantize_weights(i - 2)
-            for step in extra[1:]:
-                step()
+            for call in extra[:1]:
+                call()
             if i - 3 in last_pass:
                 finish(i - 3)
-            if i - 2 in last_pass:
-                second_product(i - 2)
+            if 1 <= i <= n_jobs:
+                quantize_weights(i - 1)
+            for call in extra[1:]:
+                call()

from contextlib import ExitStack

import concourse.mybir as mybir

H, D, NQ, N, E = 4, 128, 512, 1024, 128
FLOPS = 2 * H * N * NQ * D + 2 * H * NQ * N * E

F32 = mybir.dt.float32
BF16 = mybir.dt.bfloat16
U32 = mybir.dt.uint32
U8 = mybir.dt.uint8
FP8X4 = mybir.dt.float8_e4m3fn_x4
ACT = mybir.ActivationFunctionType
ALU = mybir.AluOpType

P = 128
PACK = 4
RUN = 4
ROWS = D // PACK
PASS = P * PACK
PASSES = N // PASS
QC = 128
CHUNKS = NQ // QC
TANH_RING = 3
SILU_RING = 4
W_RING = 3
Y_BANKS = 4


def tile_rows_a_silu_mask_cap_gate_kernel(tc, qT, kT, t, v, mask, og, out):
    nc = tc.nc
    with ExitStack() as ctx:
        sb = ctx.enter_context(tc.tile_pool(name="sb", bufs=1))
        ps = ctx.enter_context(tc.psum_pool(name="ps", bufs=1))
        ctx.enter_context(tc.manual_schedule())

        def sbuf(name, shape, dtype):
            return sb.tile(shape, dtype, name=name, align_bytes=64)

        q_hbm = qT.rearrange("h (p j) n -> (h p) j n", j=PACK)
        k_hbm = kT.rearrange("h (p j) n -> (h p) j n", j=PACK)
        m_hbm = mask.rearrange("(c p j) q -> c p j q", p=P, j=PACK)
        v_hbm = v.rearrange("h (c p j) e -> c p h (j e)", p=P, j=PACK)

        half_pass = PASS // 2
        half_q = NQ // 2
        q_first = sbuf("q_first", [P, PACK, QC], F32)
        q_rest = sbuf("q_rest", [P, PACK, NQ - QC], F32)
        k0_lo = sbuf("k0_lo", [P, PACK, half_pass], F32)
        k0_hi = sbuf("k0_hi", [P, PACK, half_pass], F32)
        k1_raw = sbuf("k1_raw", [P, PACK, PASS], F32)
        m0_lo = sbuf("m0_lo", [P, PACK, half_q], F32)
        m0_hi = sbuf("m0_hi", [P, PACK, half_q], F32)
        m1_raw = sbuf("m1_raw", [P, PACK, NQ], F32)
        v_raw = [sbuf("v_raw%d" % c, [P, H, PACK * E], F32) for c in range(PASSES)]
        og_raw = sbuf("og_raw", [P, H * CHUNKS, E], F32)
        t_sb = sbuf("t_sb", [P, PASSES, PACK], F32)

        nc.sync.dma_start(out=k0_lo[:], in_=k_hbm[:, :, 0:half_pass])
        nc.sync.dma_start(out=k0_hi[:], in_=k_hbm[:, :, half_pass:PASS])
        nc.sync.dma_start(out=q_first[:], in_=q_hbm[:, :, 0:QC])
        nc.sync.dma_start(out=t_sb[:], in_=t.rearrange("(c p j) o -> p c (j o)", p=P, j=PACK))
        nc.sync.dma_start(out=q_rest[:], in_=q_hbm[:, :, QC:NQ])
        nc.sync.dma_start(out=m0_lo[:], in_=m_hbm[0][:, :, 0:half_q])
        nc.sync.dma_start(out=m0_hi[:], in_=m_hbm[0][:, :, half_q:NQ])
        nc.sync.dma_start(out=k1_raw[:], in_=k_hbm[:, :, PASS:N])
        nc.sync.dma_start(out=m1_raw[:], in_=m_hbm[1])
        for c in range(PASSES):
            nc.sync.dma_start(out=v_raw[c][:], in_=v_hbm[c])
        nc.sync.dma_start(out=og_raw[:], in_=og.rearrange("h (c p) e -> p (h c) e", p=QC))

        q_bf = sbuf("q_bf", [P, NQ * PACK], BF16)
        k_bf = [sbuf("k_bf%d" % c, [P, PASS * PACK], BF16) for c in range(PASSES)]
        v_bf = [sbuf("v_bf%d" % c, [P, H * E * PACK], BF16) for c in range(PASSES)]
        q_codes = sbuf("q_codes", [P, NQ], U32)
        q_scales = sbuf("q_scales", [P, NQ], U8)
        k_codes = sbuf("k_codes", [P, N], U32)
        k_scales = sbuf("k_scales", [P, N], U8)
        v_codes = sbuf("v_codes", [P, PASSES * H * E], U32)
        v_scales = sbuf("v_scales", [P, PASSES * H * E], U8)
        w_codes = sbuf("w_codes", [P, PASSES * CHUNKS * H * QC], U32)
        w_scales = sbuf("w_scales", [P, PASSES * CHUNKS * H * QC], U8)
        mt_rows = sbuf("mt_rows", [P, PACK, NQ], F32)
        mt = [sbuf("mt%d" % c, [P, NQ * PACK], F32) for c in range(PASSES)]
        gate = sbuf("gate", [P, CHUNKS, H * E], F32)
        tanh_ring = [sbuf("tanh%d" % i, [P, H, QC * PACK], F32) for i in range(TANH_RING)]
        silu_ring = [sbuf("silu%d" % i, [P, H, QC * PACK], F32) for i in range(SILU_RING)]
        w_ring = [sbuf("w%d" % i, [P, H * QC * PACK], BF16) for i in range(W_RING)]
        score_bank = [ps.tile([P, PACK * QC], F32, name="score%d" % h) for h in range(H)]
        y_bank = [ps.tile([P, H * E], F32, name="y%d" % i) for i in range(Y_BANKS)]

        def quantize(codes, scales, values, first, width):
            nc.vector.quantize_mx(
                out=codes[:, first : first + width].bitcast(FP8X4),
                scales=scales[:, first : first + width],
                in_=values,
            )

        def interleave(copy, dst, src):
            copy(
                out=dst.rearrange("p (c i j) -> p c j i", i=RUN, j=PACK),
                in_=src.rearrange("p j (c i) -> p c j i", i=RUN),
            )

        def interleave_queries(copy, src, q0, q1):
            interleave(copy, q_bf[:, q0 * PACK : q1 * PACK], src)

        def quantize_queries(q0, q1):
            quantize(q_codes, q_scales, q_bf[:, q0 * PACK : q1 * PACK], q0, q1 - q0)

        def deal_keys(c, src, s0, s1):
            dst = k_bf[c][:].rearrange("p (r s j) -> p s j r", r=PACK, j=PACK)
            nc.vector.tensor_copy(out=dst[:, s0:s1], in_=src.rearrange("p j (s r) -> p s j r", r=PACK))

        def quantize_keys(c, r0, r1):
            quantize(k_codes, k_scales, k_bf[c][:, r0 * P * PACK : r1 * P * PACK], c * PASS + r0 * P, (r1 - r0) * P)

        def scale_mask(c, src, q0, q1):
            for r in range(PACK):
                nc.vector.tensor_scalar(
                    out=mt_rows[:, r, q0:q1], in0=src[:, r, :], scalar1=t_sb[:, c, r : r + 1],
                    scalar2=1.0 / 32.0, op0=ALU.mult, op1=ALU.mult,
                )

        def interleave_mask(c, q0, q1):
            interleave(nc.vector.tensor_copy, mt[c][:, q0 * PACK : q1 * PACK], mt_rows[:, :, q0:q1])

        def interleave_values(c):
            nc.vector.tensor_copy(
                out=v_bf[c][:].rearrange("p (h c i r) -> p h c r i", h=H, i=RUN, r=PACK),
                in_=v_raw[c][:].rearrange("p h (r c i) -> p h c r i", r=PACK, i=RUN),
            )

        def quantize_values(c):
            quantize(v_codes, v_scales, v_bf[c][:], c * H * E, H * E)

        units = [(c, qc, h) for c in range(PASSES) for qc in range(CHUNKS) for h in range(H)]
        sizes = [2, 2] + [H] * (PASSES * CHUNKS - 3) + [2, 2, 2, 1, 1]
        jobs = [list(range(sum(sizes[:g]), sum(sizes[: g + 1]))) for g in range(len(sizes))]

        def scores(u):
            c, qc, h = units[u]
            rows = slice(ROWS * h, ROWS * (h + 1))
            q_cols = slice(qc * QC, (qc + 1) * QC)
            for r in range(PACK):
                k_cols = slice(c * PASS + r * P, c * PASS + (r + 1) * P)
                nc.tensor.matmul_mx(
                    out=score_bank[h][:, r * QC : (r + 1) * QC],
                    lhsT=k_codes[rows, k_cols].bitcast(FP8X4), lhsT_scale=k_scales[rows, k_cols],
                    rhs=q_codes[rows, q_cols].bitcast(FP8X4), rhs_scale=q_scales[rows, q_cols],
                    start=True, stop=True,
                )

        def cap(g, member):
            h = units[jobs[g][member]][2]
            nc.scalar.activation(
                out=tanh_ring[g % TANH_RING][:, member, :].rearrange("p (n r) -> p n r", r=PACK),
                in_=score_bank[h][:].rearrange("p (r n) -> p n r", r=PACK),
                func=ACT.Tanh, scale=0.5,
            )

        def silu(g):
            n = len(jobs[g])
            nc.scalar.activation(
                out=silu_ring[g % SILU_RING][:, 0:n, :], in_=tanh_ring[g % TANH_RING][:, 0:n, :],
                func=ACT.Silu, scale=2.0,
            )

        def weigh(g):
            n = len(jobs[g])
            c, qc, h = units[jobs[g][0]]
            width = QC * PACK
            nc.vector.tensor_tensor(
                out=w_ring[g % W_RING][:, 0 : n * width].rearrange("p (a x) -> p a x", a=n),
                in0=silu_ring[g % SILU_RING][:, 0:n, :],
                in1=mt[c][:, qc * width : (qc + 1) * width].unsqueeze(1).to_broadcast([P, n, width]),
                op=ALU.mult,
            )

        def quantize_weights(g):
            n = len(jobs[g])
            quantize(w_codes, w_scales, w_ring[g % W_RING][:, 0 : n * QC * PACK], jobs[g][0] * QC, n * QC)

        def second_product(g):
            for member, u in enumerate(jobs[g]):
                qc, h = units[u][1:]
                for c in range(PASSES):
                    w0 = ((c * CHUNKS + qc) * H + h) * QC
                    v0 = (c * H + h) * E
                    nc.tensor.matmul_mx(
                        out=y_bank[g % Y_BANKS][:, member * E : (member + 1) * E],
                        lhsT=w_codes[:, w0 : w0 + QC].bitcast(FP8X4), lhsT_scale=w_scales[:, w0 : w0 + QC],
                        rhs=v_codes[:, v0 : v0 + E].bitcast(FP8X4), rhs_scale=v_scales[:, v0 : v0 + E],
                        start=(c == 0), stop=(c == PASSES - 1),
                    )

        def make_gate(g):
            n = len(jobs[g])
            c, qc, h = units[jobs[g][0]]
            nc.scalar.activation(
                out=gate[:, qc, h * E : (h + n) * E].rearrange("p (h e) -> p h e", h=n),
                in_=og_raw[:].rearrange("p (h c) e -> p c h e", h=H)[:, qc, h : h + n],
                func=ACT.Tanh, scale=0.5,
            )

        def finish(g):
            n = len(jobs[g])
            c, qc, h = units[jobs[g][0]]
            result = sbuf("result%d" % g, [P, n * E], F32)
            nc.vector.scalar_tensor_tensor(
                out=result[:], in0=gate[:, qc, h * E : (h + n) * E], scalar=1.0,
                in1=y_bank[g % Y_BANKS][:, 0 : n * E], op0=ALU.add, op1=ALU.mult,
            )
            nc.sync.dma_start(
                out=out[h : h + n, qc * QC : (qc + 1) * QC, :].rearrange("h q e -> q h e"),
                in_=result[:].rearrange("p (h e) -> p h e", h=n),
            )

        interleave_queries(nc.scalar.copy, q_first[:], 0, QC)
        deal_keys(0, k0_lo[:], 0, P // 2)
        deal_keys(0, k0_hi[:], P // 2, P)
        quantize_keys(0, 0, PACK // 2)
        quantize_keys(0, PACK // 2, PACK)
        quantize_queries(0, QC)
        for u in range(H):
            scores(u)

        interleave_queries(nc.vector.tensor_copy, q_rest[:, :, 0:QC], QC, half_q)
        interleave_queries(nc.vector.tensor_copy, q_rest[:, :, QC : NQ - QC], half_q, NQ)
        quantize_queries(QC, half_q)
        scale_mask(0, m0_lo, 0, half_q)
        quantize_queries(half_q, NQ)
        interleave_mask(0, 0, half_q)
        scale_mask(0, m0_hi, half_q, NQ)

        preparation = [
            (lambda: interleave_mask(0, half_q, NQ),),
            (lambda: deal_keys(1, k1_raw[:], 0, P), lambda: quantize_keys(1, 0, PACK)),
            (lambda: scale_mask(1, m1_raw, 0, NQ), lambda: interleave_mask(1, 0, NQ)),
            (lambda: interleave_values(0), lambda: quantize_values(0)),
            (lambda: interleave_values(1), lambda: quantize_values(1)),
        ]
        n_jobs = len(jobs)
        last_pass = [g for g in range(n_jobs) if units[jobs[g][0]][0] == PASSES - 1]

        for i in range(n_jobs + 3):
            members = range(len(jobs[i])) if i < n_jobs else range(0)
            for member in members:
                cap(i, member)
                u_next = jobs[i][member] + H
                if u_next < len(units):
                    scores(u_next)
                if member == 0 and i - 2 in last_pass:
                    second_product(i - 2)
                if member == 0 and i >= 1:
                    silu(i - 1)
            if i >= n_jobs and i - 2 in last_pass:
                second_product(i - 2)
            if i == n_jobs:
                silu(i - 1)
            if i - 3 in last_pass:
                make_gate(i - 3)
            extra = preparation[i - 1] if 1 <= i <= len(preparation) else ()
            if 1 <= i <= n_jobs:
                weigh(i - 1)
            for call in extra[:1]:
                call()
            if i - 3 in last_pass:
                finish(i - 3)
            if 1 <= i <= n_jobs:
                quantize_weights(i - 1)
            for call in extra[1:]:
                call()
